import numpy as np
import ml_dtypes


def mxq(x, axis, fmt="e4m3"):
    dtype, down = {"e4m3": (ml_dtypes.float8_e4m3fn, 7), "e5m2": (ml_dtypes.float8_e5m2, 14)}[fmt]
    v = np.moveaxis(np.asarray(x, np.float32).astype(ml_dtypes.bfloat16).astype(np.float64), axis, -1)
    blocks = v.reshape(v.shape[:-1] + (-1, 32))
    amax = np.abs(blocks).max(-1, keepdims=True)
    byte = np.maximum(np.where(amax > 0, np.frexp(amax)[1] - 1 + 127, 0) - down, 1)
    scale = np.exp2(byte - 127.0)
    codes = (blocks / scale).astype(np.float32).astype(dtype).astype(np.float64)
    return np.moveaxis((codes * scale).reshape(v.shape), -1, axis)


WIDE = False


def mx_kscale(k):
    if not WIDE:
        return np.ones(k)
    levels = np.array([10, -10, 5, -5, 0])
    if k % 512:
        return np.exp2(np.random.permutation(np.resize(levels, k // 32))).repeat(32)
    a = np.empty((k // 512, 16))
    for p in range(k // 512):
        a[p, :8] = np.random.permutation(np.resize(levels, 8))
        for g in range(8):
            far = levels[np.abs(levels - a[p, g]) >= 10]
            a[p, g + 8] = far[np.random.randint(len(far))]
    return np.exp2(a.ravel()).repeat(32)


def f64(x):
    return np.asarray(x).astype(np.float64)


def striped(idx):
    return np.tile(idx.reshape(-1, 16).T, (8, 1)).astype(np.uint16)


def unstriped(offs):
    return offs[:16].T.reshape(-1).astype(np.int64)


def pack_weight(w):
    k, n = w.shape
    w = f64(np.asarray(w, np.float32).astype(ml_dtypes.bfloat16)).reshape(k // 32, 32, n)
    amax = np.abs(w).max(1)
    byte = np.clip(np.where(amax > 0, np.frexp(amax)[1] - 1 + 127 - 7, 1), 1, 254)
    scaled = (w * np.exp2(127.0 - byte)[:, None, :]).reshape(k, n).astype(np.float32)
    words = np.ascontiguousarray(scaled.reshape(k // 512, 128, 4, n).transpose(0, 1, 3, 2)).astype(ml_dtypes.float8_e4m3fn).view(np.uint8)
    return words, np.ascontiguousarray(byte.astype(np.uint8).reshape(k // 512, 16, n))


def unpack_weight(words, scales):
    g, p, n, _ = words.shape
    vals = np.ascontiguousarray(words).view(ml_dtypes.float8_e4m3fn).astype(np.float64) * np.repeat(np.exp2(scales.astype(np.float64) - 127.0), 8, axis=1)[..., None]
    return vals.transpose(0, 1, 3, 2).reshape(g * 512, n)


K, T, S, J = 512, 2048, 512, 256


def setup_inputs():
    n = np.random.standard_normal
    s = mx_kscale(K)[:, None]
    packed_xT = pack_weight(n((K, T)) * s)
    return {
        "x_words": packed_xT[0],
        "x_scales": packed_xT[1],
        "hT": (n((K, J)) / np.sqrt(K) / s).astype(np.float32),
        "gT": (n((K, J)) / np.sqrt(K) / s).astype(np.float32),
        "offs": striped(np.random.permutation(T)[:S]),
    }


def reference(x_words, x_scales, hT, gT, offs):
    hTq = mxq(f64(hT), 0, "e4m3")
    xq = unpack_weight(x_words, x_scales)[:, unstriped(offs)]
    y = hTq.T @ xq
    e = np.exp(y - y.max(axis=1, keepdims=True))
    p = e / e.sum(axis=1, keepdims=True)
    gTq = mxq(f64(gT), 0, "e4m3")
    z = gTq.T @ xq
    e = np.exp(z - z.max(axis=1, keepdims=True))
    q = e / e.sum(axis=1, keepdims=True)
    return np.minimum(p, q)

@@ -1,0 +1,108 @@
+from contextlib import ExitStack
+
+import concourse.mybir as mybir
+
+K, T, S, J = 512, 2048, 512, 256
+FLOPS = 2 * 2 * K * S * J
+
+F32 = mybir.dt.float32
+BF16 = mybir.dt.bfloat16
+I32 = mybir.dt.int32
+U32 = mybir.dt.uint32
+U16 = mybir.dt.uint16
+U8 = mybir.dt.uint8
+FP8X4 = mybir.dt.float8_e4m3fn_x4
+ALU = mybir.AluOpType
+ACT = mybir.ActivationFunctionType
+
+P = 128
+PACK = 4
+
+
+def tile_picked_zspec_ovl_p_kernel(tc, x_words, x_scales, hT, gT, offs, out):
+    nc = tc.nc
+    with ExitStack() as ctx:
+        keep = ctx.enter_context(tc.tile_pool(name="keep", bufs=1))
+        psum = ctx.enter_context(tc.psum_pool(name="psum", bufs=1))
+
+        offsets = keep.tile([P, S // 16], U16, name="offsets")
+        nc.sync.dma_start(offsets[:], offs)
+
+        scale_table = keep.tile([P, T], U8, name="scale_table", align_bytes=64)
+        nc.vector.memset(scale_table[:].bitcast(I32), 0)
+        for q in range(4):
+            nc.scalar.dma_start(scale_table[32 * q : 32 * q + 4, :].bitcast(I32), x_scales[0, 4 * q : 4 * q + 4, :].bitcast(I32))
+
+        word_table = keep.tile([P, T], I32, name="word_table", align_bytes=64)
+        nc.sync.dma_start(word_table[:], x_words[0].rearrange("p n t -> p (n t)").bitcast(I32))
+
+        raw = {}
+        for name, src in (("h", hT), ("g", gT)):
+            raw[name] = keep.tile([P, PACK, J], F32, name="raw_" + name)
+            nc.sync.dma_start(raw[name][:], src.rearrange("(p j) w -> p j w", j=PACK))
+
+        x_scale = keep.tile([P, S], U8, name="x_scale", align_bytes=64)
+        nc.vector.tensor_copy(x_scale[:], scale_table[:].indirect(offsets[:]))
+        x_code = keep.tile([P, S], U32, name="x_code", align_bytes=64)
+        nc.vector.tensor_copy(x_code[:], word_table[:].bitcast(U32).indirect(offsets[:]))
+
+        def cast(name, m, on_scalar):
+            grouped = keep.tile([P, P, PACK], BF16, name="grouped_%s%d" % (name, m), align_bytes=64)
+            dst = grouped[:].rearrange("p (c i) j -> p c j i", i=4)
+            src = raw[name][:, :, m * P : (m + 1) * P].rearrange("p j (c i) -> p c j i", i=4)
+            if on_scalar:
+                nc.scalar.activation(dst, src, ACT.Copy)
+            else:
+                nc.vector.tensor_copy(dst, src)
+            return grouped
+
+        def logits(name, m, grouped):
+            code = keep.tile([P, P], U32, name="code_%s%d" % (name, m), align_bytes=64)
+            scale = keep.tile([P, P], U8, name="scale_%s%d" % (name, m), align_bytes=64)
+            nc.vector.quantize_mx(out=code[:].bitcast(FP8X4), scales=scale[:], in_=grouped[:].rearrange("p w j -> p (w j)"))
+            bank = psum.tile([P, S], F32, name="bank_%s%d" % (name, m))
+            nc.tensor.matmul_mx(
+                out=bank[:], lhsT=code[:].bitcast(FP8X4), lhsT_scale=scale[:],
+                rhs=x_code[:].bitcast(FP8X4), rhs_scale=x_scale[:], start=True, stop=True,
+            )
+            return bank
+
+        def exponent(name, m, bank):
+            neg_max = keep.tile([P, 1], F32, name="neg_max_%s%d" % (name, m))
+            nc.vector.tensor_reduce(neg_max[:], bank[:], mybir.AxisListType.X, ALU.max, negate=True)
+            e = keep.tile([P, S], F32, name="e_%s%d" % (name, m))
+            total = keep.tile([P, 1], F32, name="total_%s%d" % (name, m))
+            nc.scalar.activation(e[:], bank[:], ACT.Exp, bias=neg_max[:], scale=1.0, accum_out=total[:])
+            return e, total
+
+        def inverse(name, m, total):
+            inv = keep.tile([P, 1], F32, name="inv_%s%d" % (name, m))
+            nc.vector.reciprocal(inv[:], total[:])
+            return inv
+
+        gr = {}
+        gr["h", 0] = cast("h", 0, True)
+        gr["h", 1] = cast("h", 1, True)
+        gr["g", 0] = cast("g", 0, True)
+        gr["g", 1] = cast("g", 1, True)
+        banks = {}
+        ex = {}
+        prob = {}
+        for m in range(2):
+            banks["h", m] = logits("h", m, gr["h", m])
+        for m in range(2):
+            ex["h", m] = exponent("h", m, banks["h", m])
+        for m in range(2):
+            banks["g", m] = logits("g", m, gr["g", m])
+        for m in range(2):
+            ex["g", m] = exponent("g", m, banks["g", m])
+            e, total = ex["h", m]
+            inv = inverse("h", m, total)
+            prob[m] = keep.tile([P, S], F32, name="prob%d" % m)
+            nc.gpsimd.tensor_scalar(prob[m][:], e[:], inv[:], 0.0, ALU.mult, ALU.add)
+        for m in range(2):
+            e, total = ex["g", m]
+            inv = inverse("g", m, total)
+            res = keep.tile([P, S], F32, name="res%d" % m)
+            nc.vector.scalar_tensor_tensor(res[:], e[:], inv[:], prob[m][:], ALU.mult, ALU.min)
+            nc.sync.dma_start(out[m * P : (m + 1) * P, :], res[:])

@@ -25,84 +25,101 @@ def tile_picked_zspec_ovl_p_kernel(tc, x_words, x_scales, hT, gT, offs, out):
         keep = ctx.enter_context(tc.tile_pool(name="keep", bufs=1))
         psum = ctx.enter_context(tc.psum_pool(name="psum", bufs=1))
 
-        offsets = keep.tile([P, S // 16], U16, name="offsets")
-        nc.sync.dma_start(offsets[:], offs)
-
-        scale_table = keep.tile([P, T], U8, name="scale_table", align_bytes=64)
-        nc.vector.memset(scale_table[:].bitcast(I32), 0)
-        for q in range(4):
-            nc.scalar.dma_start(scale_table[32 * q : 32 * q + 4, :].bitcast(I32), x_scales[0, 4 * q : 4 * q + 4, :].bitcast(I32))
-
         word_table = keep.tile([P, T], I32, name="word_table", align_bytes=64)
-        nc.sync.dma_start(word_table[:], x_words[0].rearrange("p n t -> p (n t)").bitcast(I32))
+        words_in = x_words[0].rearrange("p n t -> p (n t)").bitcast(I32)
+        scale_table = keep.tile([P, T], U8, name="scale_table", align_bytes=64)
+        offsets = keep.tile([P, S // 16], U16, name="offsets")
+
+        nc.vector.memset(scale_table[:].bitcast(I32), 0)
+        nc.sync.dma_start(word_table[:, : T // 2], words_in[:, : T // 2])
+        nc.sync.dma_start(offsets[:], offs)
+        for q in range(4):
+            nc.sync.dma_start(scale_table[32 * q : 32 * q + 4, :].bitcast(I32), x_scales[0, 4 * q : 4 * q + 4, :].bitcast(I32))
+        nc.sync.dma_start(word_table[:, T // 2 :], words_in[:, T // 2 :])
 
         raw = {}
-        for name, src in (("h", hT), ("g", gT)):
-            raw[name] = keep.tile([P, PACK, J], F32, name="raw_" + name)
-            nc.sync.dma_start(raw[name][:], src.rearrange("(p j) w -> p j w", j=PACK))
+        for m in range(2):
+            for name, src in (("h", hT), ("g", gT)):
+                raw[name, m] = keep.tile([P, PACK, P], F32, name="raw_%s%d" % (name, m), tag="raw_%s%d" % (name, m))
+                nc.sync.dma_start(raw[name, m][:], src[:, m * P : (m + 1) * P].rearrange("(p j) w -> p j w", j=PACK))
 
         x_scale = keep.tile([P, S], U8, name="x_scale", align_bytes=64)
         nc.vector.tensor_copy(x_scale[:], scale_table[:].indirect(offsets[:]))
         x_code = keep.tile([P, S], U32, name="x_code", align_bytes=64)
         nc.vector.tensor_copy(x_code[:], word_table[:].bitcast(U32).indirect(offsets[:]))
 
-        def cast(name, m, on_scalar):
-            grouped = keep.tile([P, P, PACK], BF16, name="grouped_%s%d" % (name, m), align_bytes=64)
-            dst = grouped[:].rearrange("p (c i) j -> p c j i", i=4)
-            src = raw[name][:, :, m * P : (m + 1) * P].rearrange("p j (c i) -> p c j i", i=4)
+        def cast(name, m, grouped, on_scalar):
+            dst = grouped.rearrange("p (c i) j -> p c j i", i=4)
+            src = raw[name, m][:].rearrange("p j (c i) -> p c j i", i=4)
             if on_scalar:
                 nc.scalar.activation(dst, src, ACT.Copy)
             else:
                 nc.vector.tensor_copy(dst, src)
-            return grouped
 
-        def logits(name, m, grouped):
-            code = keep.tile([P, P], U32, name="code_%s%d" % (name, m), align_bytes=64)
-            scale = keep.tile([P, P], U8, name="scale_%s%d" % (name, m), align_bytes=64)
-            nc.vector.quantize_mx(out=code[:].bitcast(FP8X4), scales=scale[:], in_=grouped[:].rearrange("p w j -> p (w j)"))
-            bank = psum.tile([P, S], F32, name="bank_%s%d" % (name, m))
+        def quantise(label, grouped):
+            width = grouped.shape[1]
+            code = keep.tile([P, width], U32, name="code_" + label, align_bytes=64)
+            scale = keep.tile([P, width], U8, name="scale_" + label, align_bytes=64)
+            nc.vector.quantize_mx(out=code[:].bitcast(FP8X4), scales=scale[:], in_=grouped.rearrange("p w j -> p (w j)"))
+            return code, scale
+
+        def logits(label, code, scale):
+            bank = psum.tile([P, S], F32, name="bank_" + label)
             nc.tensor.matmul_mx(
-                out=bank[:], lhsT=code[:].bitcast(FP8X4), lhsT_scale=scale[:],
+                out=bank[:], lhsT=code.bitcast(FP8X4), lhsT_scale=scale,
                 rhs=x_code[:].bitcast(FP8X4), rhs_scale=x_scale[:], start=True, stop=True,
             )
             return bank
 
-        def exponent(name, m, bank):
-            neg_max = keep.tile([P, 1], F32, name="neg_max_%s%d" % (name, m))
+        def exponent(label, bank, total, max_tag=None, e_tag=None):
+            neg_max = keep.tile([P, 1], F32, name="neg_max_" + label, tag=max_tag or "neg_max_" + label, align_bytes=64)
             nc.vector.tensor_reduce(neg_max[:], bank[:], mybir.AxisListType.X, ALU.max, negate=True)
-            e = keep.tile([P, S], F32, name="e_%s%d" % (name, m))
-            total = keep.tile([P, 1], F32, name="total_%s%d" % (name, m))
-            nc.scalar.activation(e[:], bank[:], ACT.Exp, bias=neg_max[:], scale=1.0, accum_out=total[:])
-            return e, total
+            e = keep.tile([P, S], F32, name="e_" + label, tag=e_tag or "e_" + label)
+            nc.scalar.activation(e[:], bank[:], ACT.Exp, bias=neg_max[:], scale=1.0, accum_out=total)
+            return e
 
-        def inverse(name, m, total):
-            inv = keep.tile([P, 1], F32, name="inv_%s%d" % (name, m))
-            nc.vector.reciprocal(inv[:], total[:])
+        def inverse(label, total):
+            inv = keep.tile([P, total.shape[1]], F32, name="inv_" + label)
+            nc.vector.reciprocal(inv[:], total)
             return inv
 
-        gr = {}
-        gr["h", 0] = cast("h", 0, True)
-        gr["h", 1] = cast("h", 1, True)
-        gr["g", 0] = cast("g", 0, True)
-        gr["g", 1] = cast("g", 1, True)
-        banks = {}
-        ex = {}
-        prob = {}
-        for m in range(2):
-            banks["h", m] = logits("h", m, gr["h", m])
-        for m in range(2):
-            ex["h", m] = exponent("h", m, banks["h", m])
-        for m in range(2):
-            banks["g", m] = logits("g", m, gr["g", m])
-        for m in range(2):
-            ex["g", m] = exponent("g", m, banks["g", m])
-            e, total = ex["h", m]
-            inv = inverse("h", m, total)
-            prob[m] = keep.tile([P, S], F32, name="prob%d" % m)
-            nc.gpsimd.tensor_scalar(prob[m][:], e[:], inv[:], 0.0, ALU.mult, ALU.add)
-        for m in range(2):
-            e, total = ex["g", m]
-            inv = inverse("g", m, total)
-            res = keep.tile([P, S], F32, name="res%d" % m)
-            nc.vector.scalar_tensor_tensor(res[:], e[:], inv[:], prob[m][:], ALU.mult, ALU.min)
-            nc.sync.dma_start(out[m * P : (m + 1) * P, :], res[:])
+        def normalise(label, e, inv, engine):
+            prob = keep.tile([P, S], F32, name="prob_" + label)
+            engine.tensor_scalar(prob[:], e[:], inv, 0.0, ALU.mult, ALU.add)
+            return prob
+
+        def finish(m, half, e, inv, prob):
+            cols = slice(half * S // 2, (half + 1) * S // 2)
+            res = keep.tile([P, S // 2], F32, name="res%d_%d" % (m, half))
+            nc.vector.scalar_tensor_tensor(res[:], e[:, cols], inv, prob[:, cols], ALU.mult, ALU.min)
+            queue = nc.scalar if half else nc.sync
+            queue.dma_start(out[m * P : (m + 1) * P, cols], res[:])
+
+        grouped_h0 = keep.tile([P, P, PACK], BF16, name="grouped_h0", tag="grouped_0", align_bytes=64)
+        cast("h", 0, grouped_h0[:], True)
+        code, scale = quantise("h0", grouped_h0[:])
+        y0 = logits("y0", code[:], scale[:])
+        grouped_g0 = keep.tile([P, P, PACK], BF16, name="grouped_g0", tag="grouped_0", align_bytes=64)
+        cast("g", 0, grouped_g0[:], False)
+        code, scale = quantise("g0", grouped_g0[:])
+        z0 = logits("z0", code[:], scale[:])
+        grouped_1 = keep.tile([P, 2 * P, PACK], BF16, name="grouped_1", tag="grouped_1", align_bytes=64)
+        cast("h", 1, grouped_1[:, :P, :], True)
+        cast("g", 1, grouped_1[:, P:, :], True)
+
+        totals = keep.tile([P, 4], F32, name="totals")
+        e_y0 = exponent("y0", y0, totals[:, 0:1], e_tag="raw_g1")
+        code, scale = quantise("1", grouped_1[:])
+        y1 = logits("y1", code[:, :P], scale[:, :P])
+        z1 = logits("z1", code[:, P:], scale[:, P:])
+        e_z0 = exponent("z0", z0, totals[:, 1:2], max_tag="grouped_1")
+        p0 = normalise("y0", e_y0, inverse("y0", totals[:, 0:1])[:], nc.gpsimd)
+        e_y1 = exponent("y1", y1, totals[:, 2:3])
+        e_z1 = exponent("z1", z1, totals[:, 3:4])
+        inv_mid = inverse("mid", totals[:, 1:3])
+        finish(0, 0, e_z0, inv_mid[:, 0:1], p0)
+        p1 = normalise("y1", e_y1, inv_mid[:, 1:2], nc.vector)
+        inv_z1 = inverse("z1", totals[:, 3:4])
+        finish(0, 1, e_z0, inv_mid[:, 0:1], p0)
+        finish(1, 0, e_z1, inv_z1[:], p1)
+        finish(1, 1, e_z1, inv_z1[:], p1)

@@ -33,8 +33,8 @@ def tile_picked_zspec_ovl_p_kernel(tc, x_words, x_scales, hT, gT, offs, out):
         nc.vector.memset(scale_table[:].bitcast(I32), 0)
         nc.sync.dma_start(word_table[:, : T // 2], words_in[:, : T // 2])
         nc.sync.dma_start(offsets[:], offs)
-        for q in range(4):
-            nc.sync.dma_start(scale_table[32 * q : 32 * q + 4, :].bitcast(I32), x_scales[0, 4 * q : 4 * q + 4, :].bitcast(I32))
+        for r in range(4):
+            nc.sync.dma_start(scale_table[r:P:32, :].bitcast(I32), x_scales[0, r:16:4, :].bitcast(I32))
         nc.sync.dma_start(word_table[:, T // 2 :], words_in[:, T // 2 :])
 
         raw = {}
@@ -42,6 +42,11 @@ def tile_picked_zspec_ovl_p_kernel(tc, x_words, x_scales, hT, gT, offs, out):
             for name, src in (("h", hT), ("g", gT)):
                 raw[name, m] = keep.tile([P, PACK, P], F32, name="raw_%s%d" % (name, m), tag="raw_%s%d" % (name, m))
                 nc.sync.dma_start(raw[name, m][:], src[:, m * P : (m + 1) * P].rearrange("(p j) w -> p j w", j=PACK))
+
+        warm_in = keep.tile([P, 1], F32, name="warm_in")
+        nc.gpsimd.memset(warm_in[:], 0.0)
+        warm_out = keep.tile([P, 1], F32, name="warm_out")
+        nc.scalar.activation(warm_out[:], warm_in[:], ACT.Exp)
 
         x_scale = keep.tile([P, S], U8, name="x_scale", align_bytes=64)
         nc.vector.tensor_copy(x_scale[:], scale_table[:].indirect(offsets[:]))
@@ -92,34 +97,46 @@ def tile_picked_zspec_ovl_p_kernel(tc, x_words, x_scales, hT, gT, offs, out):
             cols = slice(half * S // 2, (half + 1) * S // 2)
             res = keep.tile([P, S // 2], F32, name="res%d_%d" % (m, half))
             nc.vector.scalar_tensor_tensor(res[:], e[:, cols], inv, prob[:, cols], ALU.mult, ALU.min)
-            queue = nc.scalar if half else nc.sync
+            queue = nc.scalar if half and m else nc.sync
             queue.dma_start(out[m * P : (m + 1) * P, cols], res[:])
 
-        grouped_h0 = keep.tile([P, P, PACK], BF16, name="grouped_h0", tag="grouped_0", align_bytes=64)
-        cast("h", 0, grouped_h0[:], True)
-        code, scale = quantise("h0", grouped_h0[:])
-        y0 = logits("y0", code[:], scale[:])
-        grouped_g0 = keep.tile([P, P, PACK], BF16, name="grouped_g0", tag="grouped_0", align_bytes=64)
-        cast("g", 0, grouped_g0[:], False)
-        code, scale = quantise("g0", grouped_g0[:])
-        z0 = logits("z0", code[:], scale[:])
-        grouped_1 = keep.tile([P, 2 * P, PACK], BF16, name="grouped_1", tag="grouped_1", align_bytes=64)
-        cast("h", 1, grouped_1[:, :P, :], True)
-        cast("g", 1, grouped_1[:, P:, :], True)
+        grouped = {}
 
-        totals = keep.tile([P, 4], F32, name="totals")
-        e_y0 = exponent("y0", y0, totals[:, 0:1], e_tag="raw_g1")
-        code, scale = quantise("1", grouped_1[:])
-        y1 = logits("y1", code[:, :P], scale[:, :P])
-        z1 = logits("z1", code[:, P:], scale[:, P:])
-        e_z0 = exponent("z0", z0, totals[:, 1:2], max_tag="grouped_1")
-        p0 = normalise("y0", e_y0, inverse("y0", totals[:, 0:1])[:], nc.gpsimd)
-        e_y1 = exponent("y1", y1, totals[:, 2:3])
-        e_z1 = exponent("z1", z1, totals[:, 3:4])
-        inv_mid = inverse("mid", totals[:, 1:3])
-        finish(0, 0, e_z0, inv_mid[:, 0:1], p0)
-        p1 = normalise("y1", e_y1, inv_mid[:, 1:2], nc.vector)
-        inv_z1 = inverse("z1", totals[:, 3:4])
-        finish(0, 1, e_z0, inv_mid[:, 0:1], p0)
+        def prepare(name, m, on_scalar):
+            label = "%s%d" % (name, m)
+            grouped[label] = keep.tile([P, P, PACK], BF16, name="grouped_" + label, align_bytes=64)
+            cast(name, m, grouped[label][:], on_scalar)
+
+        def product(label):
+            code, scale = quantise(label, grouped[label][:])
+            return logits(label, code[:], scale[:])
+
+        total = {}
+        for label in ("y0", "z0", "y1", "z1"):
+            total[label] = keep.tile([P, 1], F32, name="total_" + label)
+        prepare("h", 0, True)
+        prepare("g", 0, True)
+        y0 = product("h0")
+        prepare("h", 1, False)
+        prepare("g", 1, True)
+        z0 = product("g0")
+        y1 = product("h1")
+        e_y0 = exponent("y0", y0, total["y0"][:])
+        z1 = product("g1")
+        e_z0 = exponent("z0", z0, total["z0"][:])
+        e_y1 = exponent("y1", y1, total["y1"][:])
+        inv_y0 = inverse("y0", total["y0"][:])
+        e_z1 = exponent("z1", z1, total["z1"][:])
+        inv_z0 = inverse("z0", total["z0"][:])
+        p0 = normalise("y0", e_y0, inv_y0[:], nc.vector)
+        inv_y1 = inverse("y1", total["y1"][:])
+        res0 = keep.tile([P, S], F32, name="res0")
+        nc.vector.scalar_tensor_tensor(res0[:], e_z0[:], inv_z0[:], p0[:], ALU.mult, ALU.min)
+        nc.sync.dma_start(out[:P, :], res0[:])
+        p1 = keep.tile([P, S], F32, name="p1")
+        for half in range(2):
+            cols = slice(half * S // 2, (half + 1) * S // 2)
+            nc.scalar.activation(p1[:, cols], e_y1[:, cols], ACT.Copy, scale=inv_y1[:])
+        inv_z1 = inverse("z1", total["z1"][:])
         finish(1, 0, e_z1, inv_z1[:], p1)
         finish(1, 1, e_z1, inv_z1[:], p1)

@@ -37,11 +37,13 @@ def tile_picked_zspec_ovl_p_kernel(tc, x_words, x_scales, hT, gT, offs, out):
             nc.sync.dma_start(scale_table[r:P:32, :].bitcast(I32), x_scales[0, r:16:4, :].bitcast(I32))
         nc.sync.dma_start(word_table[:, T // 2 :], words_in[:, T // 2 :])
 
-        raw = {}
-        for m in range(2):
-            for name, src in (("h", hT), ("g", gT)):
-                raw[name, m] = keep.tile([P, PACK, P], F32, name="raw_%s%d" % (name, m), tag="raw_%s%d" % (name, m))
-                nc.sync.dma_start(raw[name, m][:], src[:, m * P : (m + 1) * P].rearrange("(p j) w -> p j w", j=PACK))
+        raw_h0 = keep.tile([P, PACK, P], F32, name="raw_h0")
+        nc.sync.dma_start(raw_h0[:], hT[:, :P].rearrange("(p j) w -> p j w", j=PACK))
+        raw_g = keep.tile([P, PACK, J], F32, name="raw_g")
+        nc.sync.dma_start(raw_g[:], gT.rearrange("(p j) w -> p j w", j=PACK))
+        raw_h1 = keep.tile([P, PACK, P], F32, name="raw_h1")
+        nc.sync.dma_start(raw_h1[:], hT[:, P:].rearrange("(p j) w -> p j w", j=PACK))
+        raw = {("h", 0): raw_h0[:], ("h", 1): raw_h1[:], ("g", 0): raw_g[:, :, :P], ("g", 1): raw_g[:, :, P:]}
 
         warm_in = keep.tile([P, 1], F32, name="warm_in")
         nc.gpsimd.memset(warm_in[:], 0.0)
@@ -55,7 +57,7 @@ def tile_picked_zspec_ovl_p_kernel(tc, x_words, x_scales, hT, gT, offs, out):
 
         def cast(name, m, grouped, on_scalar):
             dst = grouped.rearrange("p (c i) j -> p c j i", i=4)
-            src = raw[name, m][:].rearrange("p j (c i) -> p c j i", i=4)
+            src = raw[name, m].rearrange("p j (c i) -> p c j i", i=4)
             if on_scalar:
                 nc.scalar.activation(dst, src, ACT.Copy)
             else:
@@ -115,28 +117,28 @@ def tile_picked_zspec_ovl_p_kernel(tc, x_words, x_scales, hT, gT, offs, out):
         for label in ("y0", "z0", "y1", "z1"):
             total[label] = keep.tile([P, 1], F32, name="total_" + label)
         prepare("h", 0, True)
-        prepare("g", 0, True)
         y0 = product("h0")
-        prepare("h", 1, False)
+        prepare("g", 0, False)
         prepare("g", 1, True)
+        prepare("h", 1, True)
         z0 = product("g0")
-        y1 = product("h1")
-        e_y0 = exponent("y0", y0, total["y0"][:])
         z1 = product("g1")
+        e_y0 = exponent("y0", y0, total["y0"][:])
+        y1 = product("h1")
         e_z0 = exponent("z0", z0, total["z0"][:])
-        e_y1 = exponent("y1", y1, total["y1"][:])
-        inv_y0 = inverse("y0", total["y0"][:])
         e_z1 = exponent("z1", z1, total["z1"][:])
+        inv_y0 = inverse("y0", total["y0"][:])
+        e_y1 = exponent("y1", y1, total["y1"][:])
         inv_z0 = inverse("z0", total["z0"][:])
         p0 = normalise("y0", e_y0, inv_y0[:], nc.vector)
-        inv_y1 = inverse("y1", total["y1"][:])
+        inv_z1 = inverse("z1", total["z1"][:])
         res0 = keep.tile([P, S], F32, name="res0")
         nc.vector.scalar_tensor_tensor(res0[:], e_z0[:], inv_z0[:], p0[:], ALU.mult, ALU.min)
         nc.sync.dma_start(out[:P, :], res0[:])
-        p1 = keep.tile([P, S], F32, name="p1")
+        q1 = keep.tile([P, S], F32, name="q1")
         for half in range(2):
             cols = slice(half * S // 2, (half + 1) * S // 2)
-            nc.scalar.activation(p1[:, cols], e_y1[:, cols], ACT.Copy, scale=inv_y1[:])
-        inv_z1 = inverse("z1", total["z1"][:])
-        finish(1, 0, e_z1, inv_z1[:], p1)
-        finish(1, 1, e_z1, inv_z1[:], p1)
+            nc.scalar.activation(q1[:, cols], e_z1[:, cols], ACT.Copy, scale=inv_z1[:])
+        inv_y1 = inverse("y1", total["y1"][:])
+        finish(1, 0, e_y1, inv_y1[:], q1)
+        finish(1, 1, e_y1, inv_y1[:], q1)

@@ -41,7 +41,7 @@ def tile_picked_zspec_ovl_p_kernel(tc, x_words, x_scales, hT, gT, offs, out):
         nc.sync.dma_start(raw_h0[:], hT[:, :P].rearrange("(p j) w -> p j w", j=PACK))
         raw_g = keep.tile([P, PACK, J], F32, name="raw_g")
         nc.sync.dma_start(raw_g[:], gT.rearrange("(p j) w -> p j w", j=PACK))
-        raw_h1 = keep.tile([P, PACK, P], F32, name="raw_h1")
+        raw_h1 = keep.tile([P, PACK, P], F32, name="raw_h1", tag="raw_h1")
         nc.sync.dma_start(raw_h1[:], hT[:, P:].rearrange("(p j) w -> p j w", j=PACK))
         raw = {("h", 0): raw_h0[:], ("h", 1): raw_h1[:], ("g", 0): raw_g[:, :, :P], ("g", 1): raw_g[:, :, P:]}
 
@@ -106,7 +106,7 @@ def tile_picked_zspec_ovl_p_kernel(tc, x_words, x_scales, hT, gT, offs, out):
 
         def prepare(name, m, on_scalar):
             label = "%s%d" % (name, m)
-            grouped[label] = keep.tile([P, P, PACK], BF16, name="grouped_" + label, align_bytes=64)
+            grouped[label] = keep.tile([P, P, PACK], BF16, name="grouped_" + label, tag="grouped_" + label, align_bytes=64)
             cast(name, m, grouped[label][:], on_scalar)
 
         def product(label):
@@ -123,7 +123,7 @@ def tile_picked_zspec_ovl_p_kernel(tc, x_words, x_scales, hT, gT, offs, out):
         prepare("h", 1, True)
         z0 = product("g0")
         z1 = product("g1")
-        e_y0 = exponent("y0", y0, total["y0"][:])
+        e_y0 = exponent("y0", y0, total["y0"][:], e_tag="raw_h1", max_tag="grouped_g0")
         y1 = product("h1")
         e_z0 = exponent("z0", z0, total["z0"][:])
         e_z1 = exponent("z1", z1, total["z1"][:])

from contextlib import ExitStack

import concourse.mybir as mybir

K, T, S, J = 512, 2048, 512, 256
FLOPS = 2 * 2 * K * S * J

F32 = mybir.dt.float32
BF16 = mybir.dt.bfloat16
I32 = mybir.dt.int32
U32 = mybir.dt.uint32
U16 = mybir.dt.uint16
U8 = mybir.dt.uint8
FP8X4 = mybir.dt.float8_e4m3fn_x4
ALU = mybir.AluOpType
ACT = mybir.ActivationFunctionType

P = 128
PACK = 4


def tile_picked_zspec_ovl_p_kernel(tc, x_words, x_scales, hT, gT, offs, out):
    nc = tc.nc
    with ExitStack() as ctx:
        keep = ctx.enter_context(tc.tile_pool(name="keep", bufs=1))
        psum = ctx.enter_context(tc.psum_pool(name="psum", bufs=1))

        word_table = keep.tile([P, T], I32, name="word_table", align_bytes=64)
        words_in = x_words[0].rearrange("p n t -> p (n t)").bitcast(I32)
        scale_table = keep.tile([P, T], U8, name="scale_table", align_bytes=64)
        offsets = keep.tile([P, S // 16], U16, name="offsets")

        nc.vector.memset(scale_table[:].bitcast(I32), 0)
        nc.sync.dma_start(word_table[:, : T // 2], words_in[:, : T // 2])
        nc.sync.dma_start(offsets[:], offs)
        for r in range(4):
            nc.sync.dma_start(scale_table[r:P:32, :].bitcast(I32), x_scales[0, r:16:4, :].bitcast(I32))
        nc.sync.dma_start(word_table[:, T // 2 :], words_in[:, T // 2 :])

        raw_h0 = keep.tile([P, PACK, P], F32, name="raw_h0")
        nc.sync.dma_start(raw_h0[:], hT[:, :P].rearrange("(p j) w -> p j w", j=PACK))
        raw_g = keep.tile([P, PACK, J], F32, name="raw_g")
        nc.sync.dma_start(raw_g[:], gT.rearrange("(p j) w -> p j w", j=PACK))
        raw_h1 = keep.tile([P, PACK, P], F32, name="raw_h1", tag="raw_h1")
        nc.sync.dma_start(raw_h1[:], hT[:, P:].rearrange("(p j) w -> p j w", j=PACK))
        raw = {("h", 0): raw_h0[:], ("h", 1): raw_h1[:], ("g", 0): raw_g[:, :, :P], ("g", 1): raw_g[:, :, P:]}

        warm_in = keep.tile([P, 1], F32, name="warm_in")
        nc.gpsimd.memset(warm_in[:], 0.0)
        warm_out = keep.tile([P, 1], F32, name="warm_out")
        nc.scalar.activation(warm_out[:], warm_in[:], ACT.Exp)

        x_scale = keep.tile([P, S], U8, name="x_scale", align_bytes=64)
        nc.vector.tensor_copy(x_scale[:], scale_table[:].indirect(offsets[:]))
        x_code = keep.tile([P, S], U32, name="x_code", align_bytes=64)
        nc.vector.tensor_copy(x_code[:], word_table[:].bitcast(U32).indirect(offsets[:]))

        def cast(name, m, grouped, on_scalar):
            dst = grouped.rearrange("p (c i) j -> p c j i", i=4)
            src = raw[name, m].rearrange("p j (c i) -> p c j i", i=4)
            if on_scalar:
                nc.scalar.activation(dst, src, ACT.Copy)
            else:
                nc.vector.tensor_copy(dst, src)

        def quantise(label, grouped):
            width = grouped.shape[1]
            code = keep.tile([P, width], U32, name="code_" + label, align_bytes=64)
            scale = keep.tile([P, width], U8, name="scale_" + label, align_bytes=64)
            nc.vector.quantize_mx(out=code[:].bitcast(FP8X4), scales=scale[:], in_=grouped.rearrange("p w j -> p (w j)"))
            return code, scale

        def logits(label, code, scale):
            bank = psum.tile([P, S], F32, name="bank_" + label)
            nc.tensor.matmul_mx(
                out=bank[:], lhsT=code.bitcast(FP8X4), lhsT_scale=scale,
                rhs=x_code[:].bitcast(FP8X4), rhs_scale=x_scale[:], start=True, stop=True,
            )
            return bank

        def exponent(label, bank, total, max_tag=None, e_tag=None):
            neg_max = keep.tile([P, 1], F32, name="neg_max_" + label, tag=max_tag or "neg_max_" + label, align_bytes=64)
            nc.vector.tensor_reduce(neg_max[:], bank[:], mybir.AxisListType.X, ALU.max, negate=True)
            e = keep.tile([P, S], F32, name="e_" + label, tag=e_tag or "e_" + label)
            nc.scalar.activation(e[:], bank[:], ACT.Exp, bias=neg_max[:], scale=1.0, accum_out=total)
            return e

        def inverse(label, total):
            inv = keep.tile([P, total.shape[1]], F32, name="inv_" + label)
            nc.vector.reciprocal(inv[:], total)
            return inv

        def normalise(label, e, inv, engine):
            prob = keep.tile([P, S], F32, name="prob_" + label)
            engine.tensor_scalar(prob[:], e[:], inv, 0.0, ALU.mult, ALU.add)
            return prob

        def finish(m, half, e, inv, prob):
            cols = slice(half * S // 2, (half + 1) * S // 2)
            res = keep.tile([P, S // 2], F32, name="res%d_%d" % (m, half))
            nc.vector.scalar_tensor_tensor(res[:], e[:, cols], inv, prob[:, cols], ALU.mult, ALU.min)
            queue = nc.scalar if half and m else nc.sync
            queue.dma_start(out[m * P : (m + 1) * P, cols], res[:])

        grouped = {}

        def prepare(name, m, on_scalar):
            label = "%s%d" % (name, m)
            grouped[label] = keep.tile([P, P, PACK], BF16, name="grouped_" + label, tag="grouped_" + label, align_bytes=64)
            cast(name, m, grouped[label][:], on_scalar)

        def product(label):
            code, scale = quantise(label, grouped[label][:])
            return logits(label, code[:], scale[:])

        total = {}
        for label in ("y0", "z0", "y1", "z1"):
            total[label] = keep.tile([P, 1], F32, name="total_" + label)
        prepare("h", 0, True)
        y0 = product("h0")
        prepare("g", 0, False)
        prepare("g", 1, True)
        prepare("h", 1, True)
        z0 = product("g0")
        z1 = product("g1")
        e_y0 = exponent("y0", y0, total["y0"][:], e_tag="raw_h1", max_tag="grouped_g0")
        y1 = product("h1")
        e_z0 = exponent("z0", z0, total["z0"][:])
        e_z1 = exponent("z1", z1, total["z1"][:])
        inv_y0 = inverse("y0", total["y0"][:])
        e_y1 = exponent("y1", y1, total["y1"][:])
        inv_z0 = inverse("z0", total["z0"][:])
        p0 = normalise("y0", e_y0, inv_y0[:], nc.vector)
        inv_z1 = inverse("z1", total["z1"][:])
        res0 = keep.tile([P, S], F32, name="res0")
        nc.vector.scalar_tensor_tensor(res0[:], e_z0[:], inv_z0[:], p0[:], ALU.mult, ALU.min)
        nc.sync.dma_start(out[:P, :], res0[:])
        q1 = keep.tile([P, S], F32, name="q1")
        for half in range(2):
            cols = slice(half * S // 2, (half + 1) * S // 2)
            nc.scalar.activation(q1[:, cols], e_z1[:, cols], ACT.Copy, scale=inv_z1[:])
        inv_y1 = inverse("y1", total["y1"][:])
        finish(1, 0, e_y1, inv_y1[:], q1)
        finish(1, 1, e_y1, inv_y1[:], q1)
